import numpy as np
import ml_dtypes


def mxq(x, axis, fmt="e4m3"):
    dtype, down = {"e4m3": (ml_dtypes.float8_e4m3fn, 7), "e5m2": (ml_dtypes.float8_e5m2, 14)}[fmt]
    v = np.moveaxis(np.asarray(x, np.float32).astype(ml_dtypes.bfloat16).astype(np.float64), axis, -1)
    blocks = v.reshape(v.shape[:-1] + (-1, 32))
    amax = np.abs(blocks).max(-1, keepdims=True)
    byte = np.maximum(np.where(amax > 0, np.frexp(amax)[1] - 1 + 127, 0) - down, 1)
    scale = np.exp2(byte - 127.0)
    codes = (blocks / scale).astype(np.float32).astype(dtype).astype(np.float64)
    return np.moveaxis((codes * scale).reshape(v.shape), -1, axis)


WIDE = False


def mx_kscale(k):
    if not WIDE:
        return np.ones(k)
    levels = np.array([10, -10, 5, -5, 0])
    if k % 512:
        return np.exp2(np.random.permutation(np.resize(levels, k // 32))).repeat(32)
    a = np.empty((k // 512, 16))
    for p in range(k // 512):
        a[p, :8] = np.random.permutation(np.resize(levels, 8))
        for g in range(8):
            far = levels[np.abs(levels - a[p, g]) >= 10]
            a[p, g + 8] = far[np.random.randint(len(far))]
    return np.exp2(a.ravel()).repeat(32)


def f64(x):
    return np.asarray(x).astype(np.float64)


def striped(idx):
    return np.tile(idx.reshape(-1, 16).T, (8, 1)).astype(np.uint16)


def unstriped(offs):
    return offs[:16].T.reshape(-1).astype(np.int64)


def striped8(idx):
    return np.concatenate([x.reshape(-1, 16).T for x in idx]).astype(np.uint16)


def runs(offs, k):
    lists = np.stack([offs[16 * r : 16 * r + 16].T.reshape(-1) for r in range(8)]).astype(np.int64)
    return lists[np.arange(k) % 512 // 64]


def pack_weight(w):
    k, n = w.shape
    w = f64(np.asarray(w, np.float32).astype(ml_dtypes.bfloat16)).reshape(k // 32, 32, n)
    amax = np.abs(w).max(1)
    byte = np.clip(np.where(amax > 0, np.frexp(amax)[1] - 1 + 127 - 7, 1), 1, 254)
    scaled = (w * np.exp2(127.0 - byte)[:, None, :]).reshape(k, n).astype(np.float32)
    words = np.ascontiguousarray(scaled.reshape(k // 512, 128, 4, n).transpose(0, 1, 3, 2)).astype(ml_dtypes.float8_e4m3fn).view(np.uint8)
    return words, np.ascontiguousarray(byte.astype(np.uint8).reshape(k // 512, 16, n))


def unpack_weight(words, scales):
    g, p, n, _ = words.shape
    vals = np.ascontiguousarray(words).view(ml_dtypes.float8_e4m3fn).astype(np.float64) * np.repeat(np.exp2(scales.astype(np.float64) - 127.0), 8, axis=1)[..., None]
    return vals.transpose(0, 1, 3, 2).reshape(g * 512, n)


def sigmoid(v):
    return 1.0 / (1.0 + np.exp(-np.maximum(v, -700.0)))


K, T, S, N, H = 512, 2048, 512, 512, 512


def setup_inputs():
    n = np.random.standard_normal
    s = mx_kscale(K)[:, None]
    u = mx_kscale(H)
    packed_xT = pack_weight(n((K, T)) * s)
    return {
        "x_words": packed_xT[0],
        "x_scales": packed_xT[1],
        "w1": (n((K, H)) / np.sqrt(K) / s).astype(np.float32),
        "w2": (n((K, H)) / np.sqrt(K) / s).astype(np.float32),
        "gn": (np.random.uniform(0.5, 1.5, (H, 1)) * u[:, None]).astype(np.float32),
        "w3": (n((H, N)) / np.sqrt(H) / u[:, None]).astype(np.float32),
        "offs": striped(np.random.permutation(T)[:S]),
        "two": striped(np.random.permutation(T)[:S]),
        "own_l": striped8(np.stack([np.random.permutation(S) for _ in range(8)])),
        "foe": striped8(np.stack([np.random.permutation(S) for _ in range(8)])),
        "food": striped8(np.stack([np.random.permutation(S) for _ in range(8)])),
    }


def reference(x_words, x_scales, w1, w2, gn, w3, offs, two, own_l, foe, food):
    xq = unpack_weight(x_words, x_scales)[:, unstriped(offs)]
    y = sigmoid(mxq(f64(w1), 0, "e4m3").T @ xq)
    x_two = unpack_weight(x_words, x_scales)[:, unstriped(two)]
    c = sigmoid(mxq(f64(w2), 0, "e4m3").T @ x_two)
    z = f64(gn) * (y * (0.5 * (y[np.arange(H)[:, None], runs(own_l, H)]) - (c[np.arange(H)[:, None], runs(foe, H)]) + 1.5 * (y * (c[np.arange(H)[:, None], runs(food, H)]))))
    return mxq(f64(w3), 0, "e4m3").T @ mxq(z, 0, "e4m3")

@@ -1,0 +1,189 @@
+from contextlib import ExitStack
+
+import concourse.mybir as mybir
+
+K, T, S, H, N = 512, 2048, 512, 512, 512
+FLOPS = 2 * S * (2 * K * H + H * N)
+
+F32 = mybir.dt.float32
+BF16 = mybir.dt.bfloat16
+I32 = mybir.dt.int32
+U32 = mybir.dt.uint32
+U16 = mybir.dt.uint16
+U8 = mybir.dt.uint8
+FP8X4 = mybir.dt.float8_e4m3fn_x4
+MULT = mybir.AluOpType.mult
+ADD = mybir.AluOpType.add
+SIGMOID = mybir.ActivationFunctionType.Sigmoid
+
+P = 128
+PACK = 4
+CHUNK = 256
+
+
+def tile_picked_foodweb_none_p_kernel(
+    tc, x_words, x_scales, w1, w2, gn, w3, offs, two, own_l, foe, food, out
+):
+    nc = tc.nc
+    with ExitStack() as ctx:
+        keep = ctx.enter_context(tc.tile_pool(name="keep", bufs=1))
+        psum = ctx.enter_context(tc.psum_pool(name="psum", bufs=8))
+
+        def load_list(name, src):
+            t = keep.tile([P, S // 16], U16, name=name)
+            nc.sync.dma_start(t[:], src)
+            return t
+
+        def load_half(name, w, h):
+            rows = w.rearrange("(p j) c -> p j c", j=PACK)
+            raw = keep.tile([P, PACK, H // 2], F32, name="%s_raw%d" % (name, h))
+            nc.sync.dma_start(raw[:], rows[:, :, h * (H // 2) : (h + 1) * (H // 2)])
+            return raw
+
+        scale_table = keep.tile([P, T], U8, name="scale_table")
+        nc.vector.memset(scale_table[:].bitcast(I32), 0)
+        warm = keep.tile([P, 2], F32, name="warm")
+        nc.gpsimd.memset(warm[:, 0:1], 0.0)
+        nc.scalar.activation(warm[:, 1:2], warm[:, 0:1], SIGMOID)
+        for q in range(4):
+            nc.sync.dma_start(
+                scale_table[32 * q : 32 * q + 4, :].bitcast(I32), x_scales[0, 4 * q : 4 * q + 4, :].bitcast(I32)
+            )
+        offs_t = load_list("offs_t", offs)
+        w1_raw = [load_half("w1", w1, 0)]
+        two_t = load_list("two_t", two)
+        w1_raw.append(load_half("w1", w1, 1))
+        word_table = keep.tile([P, T], I32, name="word_table")
+        nc.sync.dma_start(word_table[:], x_words[0].rearrange("p n t -> p (n t)").bitcast(I32))
+        w2_raw = [load_half("w2", w2, 0), load_half("w2", w2, 1)]
+        gain = keep.tile([P, PACK], F32, name="gain")
+        nc.sync.dma_start(gain[:], gn.rearrange("(p t) o -> p (t o)", t=PACK))
+        food_t = load_list("food_t", food)
+        foe_t = load_list("foe_t", foe)
+        own_t = load_list("own_t", own_l)
+        w3_raw = [load_half("w3", w3, 0), load_half("w3", w3, 1)]
+
+        def pick_scales(name, lst):
+            t = keep.tile([P, S], U8, name=name, align_bytes=64)
+            nc.vector.tensor_copy(t[:], scale_table[:].indirect(lst[:]))
+            return t
+
+        def pick_words(name, lst):
+            t = keep.tile([P, S], U32, name=name, align_bytes=64)
+            nc.vector.tensor_copy(t[:], word_table[:].bitcast(U32).indirect(lst[:]))
+            return t
+
+        def deal(name, halves, copies):
+            grouped = keep.tile([P, PACK, P, PACK], BF16, name=name + "_grouped", align_bytes=64)
+            for h, raw in enumerate(halves):
+                copies[h](
+                    grouped[:, :, 64 * h : 64 * (h + 1), :].rearrange("p t m j -> p m j t"),
+                    raw[:].rearrange("p j (m t) -> p m j t", t=PACK),
+                )
+            return grouped
+
+        def quantize(name, grouped):
+            made = []
+            for t in range(PACK):
+                codes = keep.tile([P, P], U32, name="%s_codes%d" % (name, t), align_bytes=64)
+                plane = keep.tile([P, P], U8, name="%s_plane%d" % (name, t), align_bytes=64)
+                nc.vector.quantize_mx(
+                    out=codes[:].bitcast(FP8X4), scales=plane[:], in_=grouped[:, t].rearrange("p m j -> p (m j)")
+                )
+                made.append((codes, plane))
+            return made
+
+        def project(weights, words, scales):
+            banks = []
+            for codes, plane in weights:
+                bank = psum.tile([P, S], F32, name="bank")
+                nc.tensor.matmul_mx(
+                    out=bank[:], lhsT=codes[:].bitcast(FP8X4), lhsT_scale=plane[:],
+                    rhs=words[:].bitcast(FP8X4), rhs_scale=scales[:], start=True, stop=True,
+                )
+                banks.append(bank)
+            return banks
+
+        offs_scales = pick_scales("offs_scales", offs_t)
+        two_scales = pick_scales("two_scales", two_t)
+        w1_q = quantize("w1", deal("w1", w1_raw, (nc.scalar.copy, nc.scalar.copy)))
+        offs_words = pick_words("offs_words", offs_t)
+        y_banks = project(w1_q, offs_words, offs_scales)
+        two_words = pick_words("two_words", two_t)
+        w2_q = quantize("w2", deal("w2", w2_raw, (nc.scalar.copy, nc.vector.tensor_copy)))
+        c_banks = project(w2_q, two_words, two_scales)
+
+        y = []
+        gy = keep.tile([P, PACK, S], F32, name="gy")
+        for t in range(PACK):
+            y_t = keep.tile([P, S], F32, name="y%d" % t)
+            nc.scalar.activation(y_t[:], y_banks[t][:], SIGMOID)
+            y.append(y_t)
+            nc.vector.tensor_scalar(gy[:, t, :], y_t[:], gain[:, t : t + 1], 0.5, MULT, MULT)
+
+        w3_grouped = keep.tile([P, N, PACK], BF16, name="w3_grouped", align_bytes=64)
+        w3_codes = keep.tile([P, N], U32, name="w3_codes", align_bytes=64)
+        w3_plane = keep.tile([P, N], U8, name="w3_plane", align_bytes=64)
+
+        def weave_w3(h, copy):
+            copy(
+                w3_grouped[:, h * (N // 2) : (h + 1) * (N // 2), :].rearrange("p (c i) j -> p c j i", i=4),
+                w3_raw[h][:].rearrange("p j (c i) -> p c j i", i=4),
+            )
+
+        c_pre = []
+        out_rows = out.rearrange("(b p) n -> p b n", p=P)
+        for ch in range(S // CHUNK):
+            cols = slice(ch * CHUNK, (ch + 1) * CHUNK)
+            ent = slice(ch * CHUNK // 16, (ch + 1) * CHUNK // 16)
+            c_food = keep.tile([P, PACK, CHUNK], F32, name="c_food%d" % ch)
+            c_foe = keep.tile([P, PACK, CHUNK], F32, name="c_foe%d" % ch)
+            eaten = keep.tile([P, PACK, CHUNK], F32, name="eaten%d" % ch)
+            net = keep.tile([P, PACK, CHUNK], F32, name="net%d" % ch)
+            rate = keep.tile([P, PACK, CHUNK], F32, name="rate%d" % ch)
+            for t in range(PACK):
+                if ch == 0:
+                    pre = keep.tile([P, S], F32, name="c_pre%d" % t)
+                    nc.scalar.copy(pre[:], c_banks[t][:])
+                    c_pre.append(pre)
+                nc.scalar.activation(c_food[:, t, :], c_pre[t][:].indirect(food_t[:, ent]), SIGMOID)
+                nc.scalar.activation(c_foe[:, t, :], c_pre[t][:].indirect(foe_t[:, ent]), SIGMOID)
+            for t in range(PACK):
+                nc.vector.scalar_tensor_tensor(eaten[:, t, :], c_food[:, t, :], 3.0, y[t][:, cols], MULT, MULT)
+                if t > 0:
+                    nc.vector.tensor_tensor(rate[:, t - 1, :], y[t - 1][:].indirect(own_t[:, ent]), net[:, t - 1, :], ADD)
+                nc.vector.scalar_tensor_tensor(net[:, t, :], c_foe[:, t, :], -2.0, eaten[:, t, :], MULT, ADD)
+            if ch == 0:
+                weave_w3(0, nc.vector.tensor_copy)
+                weave_w3(1, nc.vector.tensor_copy)
+                nc.vector.quantize_mx(
+                    out=w3_codes[:].bitcast(FP8X4), scales=w3_plane[:], in_=w3_grouped[:].rearrange("p c j -> p (c j)")
+                )
+            nc.vector.tensor_tensor(rate[:, PACK - 1, :], y[PACK - 1][:].indirect(own_t[:, ent]), net[:, PACK - 1, :], ADD)
+            z = keep.tile([P, CHUNK, PACK], BF16, name="z%d" % ch, align_bytes=64)
+            nc.vector.tensor_tensor(
+                z[:].rearrange("p (c i) t -> p c t i", i=4),
+                rate[:].rearrange("p t (c i) -> p c t i", i=4),
+                gy[:, :, cols].rearrange("p t (c i) -> p c t i", i=4),
+                MULT,
+            )
+            z_codes = keep.tile([P, CHUNK], U32, name="z_codes%d" % ch, align_bytes=64)
+            z_plane = keep.tile([P, CHUNK], U8, name="z_plane%d" % ch, align_bytes=64)
+            nc.vector.quantize_mx(
+                out=z_codes[:].bitcast(FP8X4), scales=z_plane[:], in_=z[:].rearrange("p c t -> p (c t)")
+            )
+            for pair in range(2):
+                bank = psum.tile([P, S], F32, name="bank")
+                for b in range(2):
+                    m = slice((2 * pair + b) * P, (2 * pair + b + 1) * P)
+                    nc.tensor.matmul_mx(
+                        out=bank[:, b * CHUNK : (b + 1) * CHUNK],
+                        lhsT=w3_codes[:, m].bitcast(FP8X4), lhsT_scale=w3_plane[:, m],
+                        rhs=z_codes[:].bitcast(FP8X4), rhs_scale=z_plane[:], start=True, stop=True,
+                    )
+                res = keep.tile([P, 2, CHUNK], F32, name="res%d_%d" % (ch, pair))
+                if ch == S // CHUNK - 1 and pair == 1:
+                    nc.vector.tensor_copy(res[:].rearrange("p b n -> p (b n)"), bank[:])
+                else:
+                    nc.scalar.copy(res[:].rearrange("p b n -> p (b n)"), bank[:])
+                nc.sync.dma_start(out_rows[:, 2 * pair : 2 * pair + 2, cols], res[:])

@@ -27,6 +27,7 @@ def tile_picked_foodweb_none_p_kernel(
     nc = tc.nc
     with ExitStack() as ctx:
         keep = ctx.enter_context(tc.tile_pool(name="keep", bufs=1))
+        reuse = ctx.enter_context(tc.tile_pool(name="reuse", bufs=1))
         psum = ctx.enter_context(tc.psum_pool(name="psum", bufs=8))
 
         def load_list(name, src):
@@ -36,7 +37,10 @@ def tile_picked_foodweb_none_p_kernel(
 
         def load_half(name, w, h):
             rows = w.rearrange("(p j) c -> p j c", j=PACK)
-            raw = keep.tile([P, PACK, H // 2], F32, name="%s_raw%d" % (name, h))
+            if name == "w2":
+                raw = reuse.tile([P, PACK, H // 2], F32, name="w2_raw%d" % h, offset=h * 4096)
+            else:
+                raw = keep.tile([P, PACK, H // 2], F32, name="%s_raw%d" % (name, h))
             nc.sync.dma_start(raw[:], rows[:, :, h * (H // 2) : (h + 1) * (H // 2)])
             return raw
 
@@ -113,77 +117,114 @@ def tile_picked_foodweb_none_p_kernel(
         w2_q = quantize("w2", deal("w2", w2_raw, (nc.scalar.copy, nc.vector.tensor_copy)))
         c_banks = project(w2_q, two_words, two_scales)
 
+        half_gain = keep.tile([P, PACK], F32, name="half_gain")
+        nc.gpsimd.tensor_scalar(half_gain[:], gain[:], 0.5, 0.0, MULT, ADD)
         y = []
-        gy = keep.tile([P, PACK, S], F32, name="gy")
         for t in range(PACK):
-            y_t = keep.tile([P, S], F32, name="y%d" % t)
+            y_t = reuse.tile([P, S], F32, name="y%d" % t, offset=t * 2048)
             nc.scalar.activation(y_t[:], y_banks[t][:], SIGMOID)
             y.append(y_t)
-            nc.vector.tensor_scalar(gy[:, t, :], y_t[:], gain[:, t : t + 1], 0.5, MULT, MULT)
 
-        w3_grouped = keep.tile([P, N, PACK], BF16, name="w3_grouped", align_bytes=64)
-        w3_codes = keep.tile([P, N], U32, name="w3_codes", align_bytes=64)
-        w3_plane = keep.tile([P, N], U8, name="w3_plane", align_bytes=64)
-
-        def weave_w3(h, copy):
-            copy(
-                w3_grouped[:, h * (N // 2) : (h + 1) * (N // 2), :].rearrange("p (c i) j -> p c j i", i=4),
-                w3_raw[h][:].rearrange("p j (c i) -> p c j i", i=4),
-            )
-
-        c_pre = []
+        w3_q = {}
         out_rows = out.rearrange("(b p) n -> p b n", p=P)
-        for ch in range(S // CHUNK):
+
+        def weave_w3(h, copy, tag):
+            grouped = keep.tile([P, N // 2, PACK], BF16, name="w3_grouped%d" % h, tag=tag, align_bytes=64)
+            copy(grouped[:].rearrange("p (c i) j -> p c j i", i=4), w3_raw[h][:].rearrange("p j (c i) -> p c j i", i=4))
+            return grouped
+
+        def quantize_w3(h, grouped, tag):
+            codes = keep.tile([P, N // 2], U32, name="w3_codes%d" % h, tag=tag, align_bytes=64)
+            plane = keep.tile([P, N // 2], U8, name="w3_plane%d" % h, align_bytes=64)
+            nc.vector.quantize_mx(out=codes[:].bitcast(FP8X4), scales=plane[:], in_=grouped[:].rearrange("p c j -> p (c j)"))
+            w3_q[h] = (codes, plane)
+
+        c_pre = {}
+        eaten = keep.tile([P, 2, PACK, CHUNK], F32, name="eaten")
+        gained = keep.tile([P, 2, PACK, CHUNK], F32, name="gained")
+        rate = keep.tile([P, 2, PACK, CHUNK], F32, name="rate")
+        z_rows = [keep.tile([P, PACK, CHUNK], BF16, name="z_rows%d" % ch) for ch in range(2)]
+        items = [(0, 0), (0, 1), (1, 0), (2, 0), (3, 0), (1, 1), (2, 1), (3, 1)]
+        got = {}
+        for t, ch in items:
+            ent = slice(ch * CHUNK // 16, (ch + 1) * CHUNK // 16)
+            if t not in c_pre:
+                pre = keep.tile([P, S], F32, name="c_pre%d" % t)
+                (nc.vector.tensor_copy if t in (0,) else nc.scalar.copy)(pre[:], c_banks[t][:])
+                c_pre[t] = pre
+            c_food = keep.tile([P, CHUNK], F32, name="c_food", tag="c_food%d_%d" % (ch, t), align_bytes=64)
+            c_foe = keep.tile([P, CHUNK], F32, name="c_foe", tag="c_foe%d_%d" % (ch, t), align_bytes=64)
+            nc.scalar.activation(c_food[:], c_pre[t][:].indirect(food_t[:, ent]), SIGMOID)
+            nc.scalar.activation(c_foe[:], c_pre[t][:].indirect(foe_t[:, ent]), SIGMOID)
+            got[(t, ch)] = (c_food, c_foe)
+
+        def stage(which, n):
+            if not 0 <= n < len(items):
+                return
+            t, ch = items[n]
             cols = slice(ch * CHUNK, (ch + 1) * CHUNK)
             ent = slice(ch * CHUNK // 16, (ch + 1) * CHUNK // 16)
-            c_food = keep.tile([P, PACK, CHUNK], F32, name="c_food%d" % ch)
-            c_foe = keep.tile([P, PACK, CHUNK], F32, name="c_foe%d" % ch)
-            eaten = keep.tile([P, PACK, CHUNK], F32, name="eaten%d" % ch)
-            net = keep.tile([P, PACK, CHUNK], F32, name="net%d" % ch)
-            rate = keep.tile([P, PACK, CHUNK], F32, name="rate%d" % ch)
-            for t in range(PACK):
-                if ch == 0:
-                    pre = keep.tile([P, S], F32, name="c_pre%d" % t)
-                    nc.scalar.copy(pre[:], c_banks[t][:])
-                    c_pre.append(pre)
-                nc.scalar.activation(c_food[:, t, :], c_pre[t][:].indirect(food_t[:, ent]), SIGMOID)
-                nc.scalar.activation(c_foe[:, t, :], c_pre[t][:].indirect(foe_t[:, ent]), SIGMOID)
-            for t in range(PACK):
-                nc.vector.scalar_tensor_tensor(eaten[:, t, :], c_food[:, t, :], 3.0, y[t][:, cols], MULT, MULT)
-                if t > 0:
-                    nc.vector.tensor_tensor(rate[:, t - 1, :], y[t - 1][:].indirect(own_t[:, ent]), net[:, t - 1, :], ADD)
-                nc.vector.scalar_tensor_tensor(net[:, t, :], c_foe[:, t, :], -2.0, eaten[:, t, :], MULT, ADD)
-            if ch == 0:
-                weave_w3(0, nc.vector.tensor_copy)
-                weave_w3(1, nc.vector.tensor_copy)
-                nc.vector.quantize_mx(
-                    out=w3_codes[:].bitcast(FP8X4), scales=w3_plane[:], in_=w3_grouped[:].rearrange("p c j -> p (c j)")
+            if which == 0:
+                nc.vector.scalar_tensor_tensor(eaten[:, ch, t, :], got[(t, ch)][0][:], 3.0, y[t][:, cols], MULT, MULT)
+            elif which == 1:
+                nc.vector.tensor_tensor(gained[:, ch, t, :], y[t][:].indirect(own_t[:, ent]), eaten[:, ch, t, :], ADD)
+            elif which == 2:
+                nc.vector.scalar_tensor_tensor(
+                    rate[:, ch, t, :], got[(t, ch)][1][:], -2.0, gained[:, ch, t, :], MULT, ADD
                 )
-            nc.vector.tensor_tensor(rate[:, PACK - 1, :], y[PACK - 1][:].indirect(own_t[:, ent]), net[:, PACK - 1, :], ADD)
-            z = keep.tile([P, CHUNK, PACK], BF16, name="z%d" % ch, align_bytes=64)
-            nc.vector.tensor_tensor(
-                z[:].rearrange("p (c i) t -> p c t i", i=4),
-                rate[:].rearrange("p t (c i) -> p c t i", i=4),
-                gy[:, :, cols].rearrange("p t (c i) -> p c t i", i=4),
-                MULT,
-            )
-            z_codes = keep.tile([P, CHUNK], U32, name="z_codes%d" % ch, align_bytes=64)
-            z_plane = keep.tile([P, CHUNK], U8, name="z_plane%d" % ch, align_bytes=64)
-            nc.vector.quantize_mx(
-                out=z_codes[:].bitcast(FP8X4), scales=z_plane[:], in_=z[:].rearrange("p c t -> p (c t)")
-            )
+            else:
+                nc.vector.scalar_tensor_tensor(
+                    z_rows[ch][:, t, :], rate[:, ch, t, :], half_gain[:, t : t + 1], y[t][:, cols], MULT, MULT
+                )
+
+        def pack(ch, z_rows, parts):
+            width = CHUNK // parts
+            woven = []
+            for part in range(parts):
+                z = keep.tile([P, width, PACK], BF16, name="z%d_%d" % (ch, part), align_bytes=64)
+                nc.vector.tensor_copy(
+                    z[:].rearrange("p (c i) t -> p c t i", i=4),
+                    z_rows[:, :, part * width : (part + 1) * width].rearrange("p t (c i) -> p c t i", i=4),
+                )
+                woven.append(z)
+            packed = []
+            for part, z in enumerate(woven):
+                z_codes = keep.tile([P, width], U32, name="z_codes%d_%d" % (ch, part), align_bytes=64)
+                z_plane = keep.tile([P, width], U8, name="z_plane%d_%d" % (ch, part), align_bytes=64)
+                nc.vector.quantize_mx(
+                    out=z_codes[:].bitcast(FP8X4), scales=z_plane[:], in_=z[:].rearrange("p c t -> p (c t)")
+                )
+                packed.append((ch * CHUNK + part * width, width, z_codes, z_plane))
+            return packed
+
+        def finish(lo, width, z_codes, z_plane, copies):
             for pair in range(2):
-                bank = psum.tile([P, S], F32, name="bank")
+                bank = psum.tile([P, 2 * width], F32, name="bank")
                 for b in range(2):
-                    m = slice((2 * pair + b) * P, (2 * pair + b + 1) * P)
+                    m = slice(b * P, (b + 1) * P)
                     nc.tensor.matmul_mx(
-                        out=bank[:, b * CHUNK : (b + 1) * CHUNK],
-                        lhsT=w3_codes[:, m].bitcast(FP8X4), lhsT_scale=w3_plane[:, m],
+                        out=bank[:, b * width : (b + 1) * width],
+                        lhsT=w3_q[pair][0][:, m].bitcast(FP8X4), lhsT_scale=w3_q[pair][1][:, m],
                         rhs=z_codes[:].bitcast(FP8X4), rhs_scale=z_plane[:], start=True, stop=True,
                     )
-                res = keep.tile([P, 2, CHUNK], F32, name="res%d_%d" % (ch, pair))
-                if ch == S // CHUNK - 1 and pair == 1:
-                    nc.vector.tensor_copy(res[:].rearrange("p b n -> p (b n)"), bank[:])
-                else:
-                    nc.scalar.copy(res[:].rearrange("p b n -> p (b n)"), bank[:])
-                nc.sync.dma_start(out_rows[:, 2 * pair : 2 * pair + 2, cols], res[:])
+                res = keep.tile([P, 2, width], F32, name="res%d_%d" % (lo, pair))
+                copies[pair](res[:].rearrange("p b n -> p (b n)"), bank[:])
+                nc.sync.dma_start(out_rows[:, 2 * pair : 2 * pair + 2, lo : lo + width], res[:])
+
+
+        quantize_w3(0, weave_w3(0, nc.vector.tensor_copy, "w3_grouped0"), "w3_codes0")
+        stage(0, 0)
+        stage(1, 0)
+        for n in range(len(items)):
+            stage(0, n + 1)
+            stage(2, n)
+            if n == len(items) - 1:
+                quantize_w3(1, weave_w3(1, nc.scalar.copy, "c_food1_2"), "c_foe1_3")
+            stage(1, n + 1)
+            stage(3, n)
+            if n == 4:
+                packed0 = pack(0, z_rows[0], 1)
+        finish(*packed0[0], (nc.scalar.copy, nc.scalar.copy))
+        packed1 = pack(1, z_rows[1], 2)
+        finish(*packed1[0], (nc.scalar.copy, nc.vector.tensor_copy))
+        finish(*packed1[1], (nc.scalar.copy, nc.vector.tensor_copy))

@@ -18,7 +18,21 @@ SIGMOID = mybir.ActivationFunctionType.Sigmoid
 
 P = 128
 PACK = 4
-CHUNK = 256
+STRIPE = 16
+RUN = 4
+HALF = 256
+QUARTER = 128
+BANKS = 8
+ROW_BYTES = 4 * S
+
+PIECES = (
+    [(0, 0, HALF), (0, HALF, S)]
+    + [(t, 0, HALF) for t in range(1, PACK)]
+    + [(t, HALF, S) for t in range(1, PACK - 1)]
+    + [(PACK - 1, HALF, HALF + QUARTER), (PACK - 1, HALF + QUARTER, S)]
+)
+LAST = len(PIECES) - 1
+FIRST_HALF_DONE = PIECES.index((PACK - 1, 0, HALF))
 
 
 def tile_picked_foodweb_none_p_kernel(
@@ -28,203 +42,198 @@ def tile_picked_foodweb_none_p_kernel(
     with ExitStack() as ctx:
         keep = ctx.enter_context(tc.tile_pool(name="keep", bufs=1))
         reuse = ctx.enter_context(tc.tile_pool(name="reuse", bufs=1))
-        psum = ctx.enter_context(tc.psum_pool(name="psum", bufs=8))
+        psum = ctx.enter_context(tc.psum_pool(name="psum", bufs=BANKS))
 
         def load_list(name, src):
-            t = keep.tile([P, S // 16], U16, name=name)
-            nc.sync.dma_start(t[:], src)
-            return t
+            entries = keep.tile([P, S // STRIPE], U16, name=name)
+            nc.sync.dma_start(entries[:], src)
+            return entries
 
-        def load_half(name, w, h):
-            rows = w.rearrange("(p j) c -> p j c", j=PACK)
-            if name == "w2":
-                raw = reuse.tile([P, PACK, H // 2], F32, name="w2_raw%d" % h, offset=h * 4096)
-            else:
-                raw = keep.tile([P, PACK, H // 2], F32, name="%s_raw%d" % (name, h))
-            nc.sync.dma_start(raw[:], rows[:, :, h * (H // 2) : (h + 1) * (H // 2)])
+        def load_half(raw, w, h):
+            nc.sync.dma_start(raw[:], w.rearrange("(p j) c -> p j c", j=PACK)[:, :, h * HALF : (h + 1) * HALF])
             return raw
+
+        def kept_half(name, w, h):
+            return load_half(keep.tile([P, PACK, HALF], F32, name="%s_raw%d" % (name, h)), w, h)
 
         scale_table = keep.tile([P, T], U8, name="scale_table")
         nc.vector.memset(scale_table[:].bitcast(I32), 0)
-        warm = keep.tile([P, 2], F32, name="warm")
-        nc.gpsimd.memset(warm[:, 0:1], 0.0)
-        nc.scalar.activation(warm[:, 1:2], warm[:, 0:1], SIGMOID)
+
+        consts = keep.tile([P, 2], F32, name="consts")
+        zero, one_half = consts[:, 0:1], consts[:, 1:2]
+        nc.gpsimd.memset(zero, 0.0)
+        nc.scalar.activation(one_half, zero, SIGMOID)
+
         for q in range(4):
             nc.sync.dma_start(
                 scale_table[32 * q : 32 * q + 4, :].bitcast(I32), x_scales[0, 4 * q : 4 * q + 4, :].bitcast(I32)
             )
         offs_t = load_list("offs_t", offs)
-        w1_raw = [load_half("w1", w1, 0)]
+        w1_raw = [kept_half("w1", w1, 0)]
         two_t = load_list("two_t", two)
-        w1_raw.append(load_half("w1", w1, 1))
         word_table = keep.tile([P, T], I32, name="word_table")
         nc.sync.dma_start(word_table[:], x_words[0].rearrange("p n t -> p (n t)").bitcast(I32))
-        w2_raw = [load_half("w2", w2, 0), load_half("w2", w2, 1)]
+        w1_raw.append(kept_half("w1", w1, 1))
+        w2_raw = [
+            load_half(reuse.tile([P, PACK, HALF], F32, name="w2_raw%d" % h, offset=2 * h * ROW_BYTES), w2, h)
+            for h in range(2)
+        ]
         gain = keep.tile([P, PACK], F32, name="gain")
         nc.sync.dma_start(gain[:], gn.rearrange("(p t) o -> p (t o)", t=PACK))
         food_t = load_list("food_t", food)
         foe_t = load_list("foe_t", foe)
         own_t = load_list("own_t", own_l)
-        w3_raw = [load_half("w3", w3, 0), load_half("w3", w3, 1)]
+        w3_raw = [kept_half("w3", w3, h) for h in range(2)]
 
-        def pick_scales(name, lst):
-            t = keep.tile([P, S], U8, name=name, align_bytes=64)
-            nc.vector.tensor_copy(t[:], scale_table[:].indirect(lst[:]))
-            return t
+        def pick_scales(name, entries):
+            picked = keep.tile([P, S], U8, name=name, align_bytes=64)
+            nc.vector.tensor_copy(picked[:], scale_table[:].indirect(entries[:]))
+            return picked
 
-        def pick_words(name, lst):
-            t = keep.tile([P, S], U32, name=name, align_bytes=64)
-            nc.vector.tensor_copy(t[:], word_table[:].bitcast(U32).indirect(lst[:]))
-            return t
+        def pick_words(name, entries):
+            picked = keep.tile([P, S], U32, name=name, align_bytes=64)
+            nc.vector.tensor_copy(picked[:], word_table[:].bitcast(U32).indirect(entries[:]))
+            return picked
 
-        def deal(name, halves, copies):
-            grouped = keep.tile([P, PACK, P, PACK], BF16, name=name + "_grouped", align_bytes=64)
-            for h, raw in enumerate(halves):
+        def quantize(name, values, tag=None):
+            columns = values.shape[1]
+            codes = keep.tile([P, columns], U32, name=name + "_codes", tag=tag or name + "_codes", align_bytes=64)
+            scales = keep.tile([P, columns], U8, name=name + "_scales", align_bytes=64)
+            nc.vector.quantize_mx(out=codes[:].bitcast(FP8X4), scales=scales[:], in_=values.rearrange("p c j -> p (c j)"))
+            return codes, scales
+
+        def quantize_dealt(name, halves, copies):
+            dealt = keep.tile([P, PACK, P, PACK], BF16, name=name + "_dealt", align_bytes=64)
+            for h in range(2):
                 copies[h](
-                    grouped[:, :, 64 * h : 64 * (h + 1), :].rearrange("p t m j -> p m j t"),
-                    raw[:].rearrange("p j (m t) -> p m j t", t=PACK),
+                    dealt[:, :, h * (P // 2) : (h + 1) * (P // 2), :].rearrange("p t m j -> p m j t"),
+                    halves[h][:].rearrange("p j (m t) -> p m j t", t=PACK),
                 )
-            return grouped
+            return [quantize("%s_%d" % (name, t), dealt[:, t]) for t in range(PACK)]
 
-        def quantize(name, grouped):
-            made = []
-            for t in range(PACK):
-                codes = keep.tile([P, P], U32, name="%s_codes%d" % (name, t), align_bytes=64)
-                plane = keep.tile([P, P], U8, name="%s_plane%d" % (name, t), align_bytes=64)
-                nc.vector.quantize_mx(
-                    out=codes[:].bitcast(FP8X4), scales=plane[:], in_=grouped[:, t].rearrange("p m j -> p (m j)")
-                )
-                made.append((codes, plane))
-            return made
+        def multiply(result, stationary, moving):
+            nc.tensor.matmul_mx(
+                out=result,
+                lhsT=stationary[0].bitcast(FP8X4),
+                lhsT_scale=stationary[1],
+                rhs=moving[0].bitcast(FP8X4),
+                rhs_scale=moving[1],
+                start=True,
+                stop=True,
+            )
 
         def project(weights, words, scales):
             banks = []
-            for codes, plane in weights:
+            for codes, weight_scales in weights:
                 bank = psum.tile([P, S], F32, name="bank")
-                nc.tensor.matmul_mx(
-                    out=bank[:], lhsT=codes[:].bitcast(FP8X4), lhsT_scale=plane[:],
-                    rhs=words[:].bitcast(FP8X4), rhs_scale=scales[:], start=True, stop=True,
-                )
+                multiply(bank[:], (codes[:], weight_scales[:]), (words[:], scales[:]))
                 banks.append(bank)
             return banks
 
+        def interleave(name, rows, copy, tag=None):
+            woven = keep.tile([P, rows.shape[2], PACK], BF16, name=name, tag=tag or name, align_bytes=64)
+            copy(
+                woven[:].rearrange("p (c i) j -> p c j i", i=RUN), rows.rearrange("p j (c i) -> p c j i", i=RUN)
+            )
+            return woven[:]
+
         offs_scales = pick_scales("offs_scales", offs_t)
         two_scales = pick_scales("two_scales", two_t)
-        w1_q = quantize("w1", deal("w1", w1_raw, (nc.scalar.copy, nc.scalar.copy)))
+        w1_q = quantize_dealt("w1", w1_raw, (nc.scalar.copy, nc.scalar.copy))
         offs_words = pick_words("offs_words", offs_t)
         y_banks = project(w1_q, offs_words, offs_scales)
         two_words = pick_words("two_words", two_t)
-        w2_q = quantize("w2", deal("w2", w2_raw, (nc.scalar.copy, nc.vector.tensor_copy)))
+        w2_q = quantize_dealt("w2", w2_raw, (nc.scalar.copy, nc.vector.tensor_copy))
         c_banks = project(w2_q, two_words, two_scales)
 
         half_gain = keep.tile([P, PACK], F32, name="half_gain")
-        nc.gpsimd.tensor_scalar(half_gain[:], gain[:], 0.5, 0.0, MULT, ADD)
+        nc.gpsimd.tensor_scalar(half_gain[:], gain[:], one_half, 0.0, MULT, ADD)
+
         y = []
         for t in range(PACK):
-            y_t = reuse.tile([P, S], F32, name="y%d" % t, offset=t * 2048)
+            y_t = reuse.tile([P, S], F32, name="y%d" % t, offset=t * ROW_BYTES)
             nc.scalar.activation(y_t[:], y_banks[t][:], SIGMOID)
             y.append(y_t)
 
-        w3_q = {}
-        out_rows = out.rearrange("(b p) n -> p b n", p=P)
+        eaten = keep.tile([P, PACK, S], F32, name="eaten")
+        gained = keep.tile([P, PACK, S], F32, name="gained")
+        rate = keep.tile([P, PACK, S], F32, name="rate")
+        z_rows = [keep.tile([P, PACK, HALF], BF16, name="z_rows%d" % h) for h in range(2)]
 
-        def weave_w3(h, copy, tag):
-            grouped = keep.tile([P, N // 2, PACK], BF16, name="w3_grouped%d" % h, tag=tag, align_bytes=64)
-            copy(grouped[:].rearrange("p (c i) j -> p c j i", i=4), w3_raw[h][:].rearrange("p j (c i) -> p c j i", i=4))
-            return grouped
+        def entry_columns(lo, hi):
+            return slice(lo // STRIPE, hi // STRIPE)
 
-        def quantize_w3(h, grouped, tag):
-            codes = keep.tile([P, N // 2], U32, name="w3_codes%d" % h, tag=tag, align_bytes=64)
-            plane = keep.tile([P, N // 2], U8, name="w3_plane%d" % h, align_bytes=64)
-            nc.vector.quantize_mx(out=codes[:].bitcast(FP8X4), scales=plane[:], in_=grouped[:].rearrange("p c j -> p (c j)"))
-            w3_q[h] = (codes, plane)
+        def z_columns(lo, hi):
+            return z_rows[lo // HALF][:, :, lo % HALF : lo % HALF + hi - lo]
 
         c_pre = {}
-        eaten = keep.tile([P, 2, PACK, CHUNK], F32, name="eaten")
-        gained = keep.tile([P, 2, PACK, CHUNK], F32, name="gained")
-        rate = keep.tile([P, 2, PACK, CHUNK], F32, name="rate")
-        z_rows = [keep.tile([P, PACK, CHUNK], BF16, name="z_rows%d" % ch) for ch in range(2)]
-        items = [(0, 0), (0, 1), (1, 0), (2, 0), (3, 0), (1, 1), (2, 1), (3, 1)]
-        got = {}
-        for t, ch in items:
-            ent = slice(ch * CHUNK // 16, (ch + 1) * CHUNK // 16)
+        c_food, c_foe = [], []
+        for n, (t, lo, hi) in enumerate(PIECES):
             if t not in c_pre:
-                pre = keep.tile([P, S], F32, name="c_pre%d" % t)
-                (nc.vector.tensor_copy if t in (0,) else nc.scalar.copy)(pre[:], c_banks[t][:])
-                c_pre[t] = pre
-            c_food = keep.tile([P, CHUNK], F32, name="c_food", tag="c_food%d_%d" % (ch, t), align_bytes=64)
-            c_foe = keep.tile([P, CHUNK], F32, name="c_foe", tag="c_foe%d_%d" % (ch, t), align_bytes=64)
-            nc.scalar.activation(c_food[:], c_pre[t][:].indirect(food_t[:, ent]), SIGMOID)
-            nc.scalar.activation(c_foe[:], c_pre[t][:].indirect(foe_t[:, ent]), SIGMOID)
-            got[(t, ch)] = (c_food, c_foe)
+                c_pre[t] = keep.tile([P, S], F32, name="c_pre%d" % t)
+                (nc.vector.tensor_copy if t == 0 else nc.scalar.copy)(c_pre[t][:], c_banks[t][:])
+            c_food.append(keep.tile([P, hi - lo], F32, name="c_food", tag="c_food%d" % n, align_bytes=64))
+            c_foe.append(keep.tile([P, hi - lo], F32, name="c_foe", tag="c_foe%d" % n, align_bytes=64))
+            nc.scalar.activation(c_food[n][:], c_pre[t][:].indirect(food_t[:, entry_columns(lo, hi)]), SIGMOID)
+            nc.scalar.activation(c_foe[n][:], c_pre[t][:].indirect(foe_t[:, entry_columns(lo, hi)]), SIGMOID)
 
-        def stage(which, n):
-            if not 0 <= n < len(items):
-                return
-            t, ch = items[n]
-            cols = slice(ch * CHUNK, (ch + 1) * CHUNK)
-            ent = slice(ch * CHUNK // 16, (ch + 1) * CHUNK // 16)
-            if which == 0:
-                nc.vector.scalar_tensor_tensor(eaten[:, ch, t, :], got[(t, ch)][0][:], 3.0, y[t][:, cols], MULT, MULT)
-            elif which == 1:
-                nc.vector.tensor_tensor(gained[:, ch, t, :], y[t][:].indirect(own_t[:, ent]), eaten[:, ch, t, :], ADD)
-            elif which == 2:
-                nc.vector.scalar_tensor_tensor(
-                    rate[:, ch, t, :], got[(t, ch)][1][:], -2.0, gained[:, ch, t, :], MULT, ADD
-                )
-            else:
-                nc.vector.scalar_tensor_tensor(
-                    z_rows[ch][:, t, :], rate[:, ch, t, :], half_gain[:, t : t + 1], y[t][:, cols], MULT, MULT
-                )
+        def eat(n):
+            t, lo, hi = PIECES[n]
+            nc.vector.scalar_tensor_tensor(eaten[:, t, lo:hi], c_food[n][:], 3.0, y[t][:, lo:hi], MULT, MULT)
 
-        def pack(ch, z_rows, parts):
-            width = CHUNK // parts
-            woven = []
-            for part in range(parts):
-                z = keep.tile([P, width, PACK], BF16, name="z%d_%d" % (ch, part), align_bytes=64)
-                nc.vector.tensor_copy(
-                    z[:].rearrange("p (c i) t -> p c t i", i=4),
-                    z_rows[:, :, part * width : (part + 1) * width].rearrange("p t (c i) -> p c t i", i=4),
-                )
-                woven.append(z)
-            packed = []
-            for part, z in enumerate(woven):
-                z_codes = keep.tile([P, width], U32, name="z_codes%d_%d" % (ch, part), align_bytes=64)
-                z_plane = keep.tile([P, width], U8, name="z_plane%d_%d" % (ch, part), align_bytes=64)
-                nc.vector.quantize_mx(
-                    out=z_codes[:].bitcast(FP8X4), scales=z_plane[:], in_=z[:].rearrange("p c t -> p (c t)")
-                )
-                packed.append((ch * CHUNK + part * width, width, z_codes, z_plane))
-            return packed
+        def add_own(n):
+            t, lo, hi = PIECES[n]
+            looked_up = y[t][:].indirect(own_t[:, entry_columns(lo, hi)])
+            nc.vector.tensor_tensor(gained[:, t, lo:hi], looked_up, eaten[:, t, lo:hi], ADD)
 
-        def finish(lo, width, z_codes, z_plane, copies):
-            for pair in range(2):
+        def take_foe(n):
+            t, lo, hi = PIECES[n]
+            nc.vector.scalar_tensor_tensor(rate[:, t, lo:hi], c_foe[n][:], -2.0, gained[:, t, lo:hi], MULT, ADD)
+
+        def round_z(n):
+            t, lo, hi = PIECES[n]
+            nc.vector.scalar_tensor_tensor(
+                z_columns(lo, hi)[:, t, :], rate[:, t, lo:hi], half_gain[:, t : t + 1], y[t][:, lo:hi], MULT, MULT
+            )
+
+        def weave_z(lo, hi):
+            return interleave("z%d" % lo, z_columns(lo, hi), nc.vector.tensor_copy)
+
+        w3_q = [quantize("w3_0", interleave("w3_woven0", w3_raw[0][:], nc.vector.tensor_copy))]
+        z_q = []
+        eat(0)
+        add_own(0)
+        for n in range(LAST):
+            eat(n + 1)
+            take_foe(n)
+            if n == LAST - 1:
+                woven = interleave("w3_woven1", w3_raw[1][:], nc.scalar.copy, "c_food%d" % (n - 1))
+                w3_q.append(quantize("w3_1", woven, "c_foe%d" % n))
+            add_own(n + 1)
+            round_z(n)
+            if n == FIRST_HALF_DONE:
+                z_q.append(quantize("z0", weave_z(0, HALF)))
+        take_foe(LAST)
+        third_quarter = weave_z(HALF, HALF + QUARTER)
+        round_z(LAST)
+        z_q.append(quantize("z1", third_quarter))
+        z_q.append(quantize("z2", weave_z(HALF + QUARTER, S)))
+
+        out_rows = out.rearrange("(b p) n -> p b n", p=P)
+        lo = 0
+        for z_codes, z_scales in z_q:
+            width = z_codes[:].shape[1]
+            for h, (codes, weight_scales) in enumerate(w3_q):
                 bank = psum.tile([P, 2 * width], F32, name="bank")
                 for b in range(2):
                     m = slice(b * P, (b + 1) * P)
-                    nc.tensor.matmul_mx(
-                        out=bank[:, b * width : (b + 1) * width],
-                        lhsT=w3_q[pair][0][:, m].bitcast(FP8X4), lhsT_scale=w3_q[pair][1][:, m],
-                        rhs=z_codes[:].bitcast(FP8X4), rhs_scale=z_plane[:], start=True, stop=True,
+                    multiply(
+                        bank[:, b * width : (b + 1) * width],
+                        (codes[:, m], weight_scales[:, m]),
+                        (z_codes[:], z_scales[:]),
                     )
-                res = keep.tile([P, 2, width], F32, name="res%d_%d" % (lo, pair))
-                copies[pair](res[:].rearrange("p b n -> p (b n)"), bank[:])
-                nc.sync.dma_start(out_rows[:, 2 * pair : 2 * pair + 2, lo : lo + width], res[:])
-
-
-        quantize_w3(0, weave_w3(0, nc.vector.tensor_copy, "w3_grouped0"), "w3_codes0")
-        stage(0, 0)
-        stage(1, 0)
-        for n in range(len(items)):
-            stage(0, n + 1)
-            stage(2, n)
-            if n == len(items) - 1:
-                quantize_w3(1, weave_w3(1, nc.scalar.copy, "c_food1_2"), "c_foe1_3")
-            stage(1, n + 1)
-            stage(3, n)
-            if n == 4:
-                packed0 = pack(0, z_rows[0], 1)
-        finish(*packed0[0], (nc.scalar.copy, nc.scalar.copy))
-        packed1 = pack(1, z_rows[1], 2)
-        finish(*packed1[0], (nc.scalar.copy, nc.vector.tensor_copy))
-        finish(*packed1[1], (nc.scalar.copy, nc.vector.tensor_copy))
+                result = keep.tile([P, 2, width], F32, name="result%d_%d" % (lo, h))
+                copy = nc.vector.tensor_copy if (lo + width, h) == (S, 1) else nc.scalar.copy
+                copy(result[:].rearrange("p b n -> p (b n)"), bank[:])
+                nc.sync.dma_start(out_rows[:, 2 * h : 2 * h + 2, lo : lo + width], result[:])
+            lo = lo + width

from contextlib import ExitStack

import concourse.mybir as mybir

K, T, S, H, N = 512, 2048, 512, 512, 512
FLOPS = 2 * S * (2 * K * H + H * N)

F32 = mybir.dt.float32
BF16 = mybir.dt.bfloat16
I32 = mybir.dt.int32
U32 = mybir.dt.uint32
U16 = mybir.dt.uint16
U8 = mybir.dt.uint8
FP8X4 = mybir.dt.float8_e4m3fn_x4
MULT = mybir.AluOpType.mult
ADD = mybir.AluOpType.add
SIGMOID = mybir.ActivationFunctionType.Sigmoid

P = 128
PACK = 4
STRIPE = 16
RUN = 4
HALF = 256
QUARTER = 128
BANKS = 8
ROW_BYTES = 4 * S

PIECES = (
    [(0, 0, HALF), (0, HALF, S)]
    + [(t, 0, HALF) for t in range(1, PACK)]
    + [(t, HALF, S) for t in range(1, PACK - 1)]
    + [(PACK - 1, HALF, HALF + QUARTER), (PACK - 1, HALF + QUARTER, S)]
)
LAST = len(PIECES) - 1
FIRST_HALF_DONE = PIECES.index((PACK - 1, 0, HALF))


def tile_picked_foodweb_none_p_kernel(
    tc, x_words, x_scales, w1, w2, gn, w3, offs, two, own_l, foe, food, out
):
    nc = tc.nc
    with ExitStack() as ctx:
        keep = ctx.enter_context(tc.tile_pool(name="keep", bufs=1))
        reuse = ctx.enter_context(tc.tile_pool(name="reuse", bufs=1))
        psum = ctx.enter_context(tc.psum_pool(name="psum", bufs=BANKS))

        def load_list(name, src):
            entries = keep.tile([P, S // STRIPE], U16, name=name)
            nc.sync.dma_start(entries[:], src)
            return entries

        def load_half(raw, w, h):
            nc.sync.dma_start(raw[:], w.rearrange("(p j) c -> p j c", j=PACK)[:, :, h * HALF : (h + 1) * HALF])
            return raw

        def kept_half(name, w, h):
            return load_half(keep.tile([P, PACK, HALF], F32, name="%s_raw%d" % (name, h)), w, h)

        scale_table = keep.tile([P, T], U8, name="scale_table")
        nc.vector.memset(scale_table[:].bitcast(I32), 0)

        consts = keep.tile([P, 2], F32, name="consts")
        zero, one_half = consts[:, 0:1], consts[:, 1:2]
        nc.gpsimd.memset(zero, 0.0)
        nc.scalar.activation(one_half, zero, SIGMOID)

        for q in range(4):
            nc.sync.dma_start(
                scale_table[32 * q : 32 * q + 4, :].bitcast(I32), x_scales[0, 4 * q : 4 * q + 4, :].bitcast(I32)
            )
        offs_t = load_list("offs_t", offs)
        w1_raw = [kept_half("w1", w1, 0)]
        two_t = load_list("two_t", two)
        word_table = keep.tile([P, T], I32, name="word_table")
        nc.sync.dma_start(word_table[:], x_words[0].rearrange("p n t -> p (n t)").bitcast(I32))
        w1_raw.append(kept_half("w1", w1, 1))
        w2_raw = [
            load_half(reuse.tile([P, PACK, HALF], F32, name="w2_raw%d" % h, offset=2 * h * ROW_BYTES), w2, h)
            for h in range(2)
        ]
        gain = keep.tile([P, PACK], F32, name="gain")
        nc.sync.dma_start(gain[:], gn.rearrange("(p t) o -> p (t o)", t=PACK))
        food_t = load_list("food_t", food)
        foe_t = load_list("foe_t", foe)
        own_t = load_list("own_t", own_l)
        w3_raw = [kept_half("w3", w3, h) for h in range(2)]

        def pick_scales(name, entries):
            picked = keep.tile([P, S], U8, name=name, align_bytes=64)
            nc.vector.tensor_copy(picked[:], scale_table[:].indirect(entries[:]))
            return picked

        def pick_words(name, entries):
            picked = keep.tile([P, S], U32, name=name, align_bytes=64)
            nc.vector.tensor_copy(picked[:], word_table[:].bitcast(U32).indirect(entries[:]))
            return picked

        def quantize(name, values, tag=None):
            columns = values.shape[1]
            codes = keep.tile([P, columns], U32, name=name + "_codes", tag=tag or name + "_codes", align_bytes=64)
            scales = keep.tile([P, columns], U8, name=name + "_scales", align_bytes=64)
            nc.vector.quantize_mx(out=codes[:].bitcast(FP8X4), scales=scales[:], in_=values.rearrange("p c j -> p (c j)"))
            return codes, scales

        def quantize_dealt(name, halves, copies):
            dealt = keep.tile([P, PACK, P, PACK], BF16, name=name + "_dealt", align_bytes=64)
            for h in range(2):
                copies[h](
                    dealt[:, :, h * (P // 2) : (h + 1) * (P // 2), :].rearrange("p t m j -> p m j t"),
                    halves[h][:].rearrange("p j (m t) -> p m j t", t=PACK),
                )
            return [quantize("%s_%d" % (name, t), dealt[:, t]) for t in range(PACK)]

        def multiply(result, stationary, moving):
            nc.tensor.matmul_mx(
                out=result,
                lhsT=stationary[0].bitcast(FP8X4),
                lhsT_scale=stationary[1],
                rhs=moving[0].bitcast(FP8X4),
                rhs_scale=moving[1],
                start=True,
                stop=True,
            )

        def project(weights, words, scales):
            banks = []
            for codes, weight_scales in weights:
                bank = psum.tile([P, S], F32, name="bank")
                multiply(bank[:], (codes[:], weight_scales[:]), (words[:], scales[:]))
                banks.append(bank)
            return banks

        def interleave(name, rows, copy, tag=None):
            woven = keep.tile([P, rows.shape[2], PACK], BF16, name=name, tag=tag or name, align_bytes=64)
            copy(
                woven[:].rearrange("p (c i) j -> p c j i", i=RUN), rows.rearrange("p j (c i) -> p c j i", i=RUN)
            )
            return woven[:]

        offs_scales = pick_scales("offs_scales", offs_t)
        two_scales = pick_scales("two_scales", two_t)
        w1_q = quantize_dealt("w1", w1_raw, (nc.scalar.copy, nc.scalar.copy))
        offs_words = pick_words("offs_words", offs_t)
        y_banks = project(w1_q, offs_words, offs_scales)
        two_words = pick_words("two_words", two_t)
        w2_q = quantize_dealt("w2", w2_raw, (nc.scalar.copy, nc.vector.tensor_copy))
        c_banks = project(w2_q, two_words, two_scales)

        half_gain = keep.tile([P, PACK], F32, name="half_gain")
        nc.gpsimd.tensor_scalar(half_gain[:], gain[:], one_half, 0.0, MULT, ADD)

        y = []
        for t in range(PACK):
            y_t = reuse.tile([P, S], F32, name="y%d" % t, offset=t * ROW_BYTES)
            nc.scalar.activation(y_t[:], y_banks[t][:], SIGMOID)
            y.append(y_t)

        eaten = keep.tile([P, PACK, S], F32, name="eaten")
        gained = keep.tile([P, PACK, S], F32, name="gained")
        rate = keep.tile([P, PACK, S], F32, name="rate")
        z_rows = [keep.tile([P, PACK, HALF], BF16, name="z_rows%d" % h) for h in range(2)]

        def entry_columns(lo, hi):
            return slice(lo // STRIPE, hi // STRIPE)

        def z_columns(lo, hi):
            return z_rows[lo // HALF][:, :, lo % HALF : lo % HALF + hi - lo]

        c_pre = {}
        c_food, c_foe = [], []
        for n, (t, lo, hi) in enumerate(PIECES):
            if t not in c_pre:
                c_pre[t] = keep.tile([P, S], F32, name="c_pre%d" % t)
                (nc.vector.tensor_copy if t == 0 else nc.scalar.copy)(c_pre[t][:], c_banks[t][:])
            c_food.append(keep.tile([P, hi - lo], F32, name="c_food", tag="c_food%d" % n, align_bytes=64))
            c_foe.append(keep.tile([P, hi - lo], F32, name="c_foe", tag="c_foe%d" % n, align_bytes=64))
            nc.scalar.activation(c_food[n][:], c_pre[t][:].indirect(food_t[:, entry_columns(lo, hi)]), SIGMOID)
            nc.scalar.activation(c_foe[n][:], c_pre[t][:].indirect(foe_t[:, entry_columns(lo, hi)]), SIGMOID)

        def eat(n):
            t, lo, hi = PIECES[n]
            nc.vector.scalar_tensor_tensor(eaten[:, t, lo:hi], c_food[n][:], 3.0, y[t][:, lo:hi], MULT, MULT)

        def add_own(n):
            t, lo, hi = PIECES[n]
            looked_up = y[t][:].indirect(own_t[:, entry_columns(lo, hi)])
            nc.vector.tensor_tensor(gained[:, t, lo:hi], looked_up, eaten[:, t, lo:hi], ADD)

        def take_foe(n):
            t, lo, hi = PIECES[n]
            nc.vector.scalar_tensor_tensor(rate[:, t, lo:hi], c_foe[n][:], -2.0, gained[:, t, lo:hi], MULT, ADD)

        def round_z(n):
            t, lo, hi = PIECES[n]
            nc.vector.scalar_tensor_tensor(
                z_columns(lo, hi)[:, t, :], rate[:, t, lo:hi], half_gain[:, t : t + 1], y[t][:, lo:hi], MULT, MULT
            )

        def weave_z(lo, hi):
            return interleave("z%d" % lo, z_columns(lo, hi), nc.vector.tensor_copy)

        w3_q = [quantize("w3_0", interleave("w3_woven0", w3_raw[0][:], nc.vector.tensor_copy))]
        z_q = []
        eat(0)
        add_own(0)
        for n in range(LAST):
            eat(n + 1)
            take_foe(n)
            if n == LAST - 1:
                woven = interleave("w3_woven1", w3_raw[1][:], nc.scalar.copy, "c_food%d" % (n - 1))
                w3_q.append(quantize("w3_1", woven, "c_foe%d" % n))
            add_own(n + 1)
            round_z(n)
            if n == FIRST_HALF_DONE:
                z_q.append(quantize("z0", weave_z(0, HALF)))
        take_foe(LAST)
        third_quarter = weave_z(HALF, HALF + QUARTER)
        round_z(LAST)
        z_q.append(quantize("z1", third_quarter))
        z_q.append(quantize("z2", weave_z(HALF + QUARTER, S)))

        out_rows = out.rearrange("(b p) n -> p b n", p=P)
        lo = 0
        for z_codes, z_scales in z_q:
            width = z_codes[:].shape[1]
            for h, (codes, weight_scales) in enumerate(w3_q):
                bank = psum.tile([P, 2 * width], F32, name="bank")
                for b in range(2):
                    m = slice(b * P, (b + 1) * P)
                    multiply(
                        bank[:, b * width : (b + 1) * width],
                        (codes[:, m], weight_scales[:, m]),
                        (z_codes[:], z_scales[:]),
                    )
                result = keep.tile([P, 2, width], F32, name="result%d_%d" % (lo, h))
                copy = nc.vector.tensor_copy if (lo + width, h) == (S, 1) else nc.scalar.copy
                copy(result[:].rearrange("p b n -> p (b n)"), bank[:])
                nc.sync.dma_start(out_rows[:, 2 * h : 2 * h + 2, lo : lo + width], result[:])
            lo = lo + width
